import numpy as np
import ml_dtypes

BF16 = ml_dtypes.bfloat16


def bf(x):
    return np.asarray(x, np.float32).astype(BF16)


def f32(x):
    return np.asarray(x, np.float32)


def f64(x):
    return np.asarray(x).astype(np.float64)


def striped(idx):
    return np.tile(idx.reshape(-1, 16).T, (8, 1))


def rows(idx, k):
    return np.tile(idx, (k, 1))


def look(tab, idx):
    return np.take_along_axis(f64(tab), rows(idx, len(tab)), axis=1)


K, S, V, N, M = 128, 256, 128, 128, 256


def setup_inputs():
    return {"tab": f32(np.random.standard_normal((2, K, S))), "w": bf(np.random.standard_normal((K, M)) / np.sqrt(K)), "b": f32(0.5 * np.random.standard_normal((M, 1))), "offs": striped(np.random.permutation(S)[:N])}


def reference(tab, w, b, offs):
    idx = offs[:16].T.reshape(-1)
    x = 1.0 / (1.0 + np.exp(-look(tab[0], idx))) * np.tanh(look(tab[1], idx))
    y = f64(w).T @ x
    return np.maximum(y + f64(b), 0.0)

@@ -1,0 +1,44 @@
+import concourse.mybir as mybir
+
+F32, BF16, U16 = mybir.dt.float32, mybir.dt.bfloat16, mybir.dt.uint16
+ADD, MAX, MULT = mybir.AluOpType.add, mybir.AluOpType.max, mybir.AluOpType.mult
+SIGMOID = mybir.ActivationFunctionType.Sigmoid
+TANH = mybir.ActivationFunctionType.Tanh
+RELU = mybir.ActivationFunctionType.Relu
+
+R, S, N, M = 128, 256, 128, 256
+BLOCKS = M // 128
+FLOPS = 2 * R * M * N
+
+
+def tile_lookup_cell_sigtanh_relu_kernel(tc, tab, w, b, offs, out):
+    nc = tc.nc
+    with tc.tile_pool(name="held", bufs=1) as held, tc.psum_pool(name="psum", bufs=1) as psum:
+        offsets = held.tile([128, N // 16], U16, name="offsets")
+        gate = held.tile([R, S], F32, name="gate")
+        state = held.tile([R, S], F32, name="state")
+        weights = held.tile([R, M], BF16, name="weights")
+        bias = held.tile([128, BLOCKS], F32, name="bias")
+        nc.sync.dma_start(offsets[:], offs)
+        nc.sync.dma_start(gate[:], tab[0])
+        nc.sync.dma_start(state[:], tab[1])
+        nc.sync.dma_start(weights[:], w)
+        nc.sync.dma_start(bias[:], b.rearrange("(p k) o -> p (k o)", k=BLOCKS))
+
+        opened = held.tile([R, N], F32, name="opened")
+        squashed = held.tile([R, N], F32, name="squashed")
+        nc.scalar.activation(opened[:], gate[:].indirect(offsets[:]), SIGMOID)
+        nc.scalar.activation(squashed[:], state[:].indirect(offsets[:]), TANH)
+        x = held.tile([R, N], BF16, name="x")
+        nc.vector.tensor_tensor(x[:], opened[:], squashed[:], MULT)
+
+        weights_of_block = weights[:].rearrange("r (p k) -> r k p", k=BLOCKS)
+        result = held.tile([128, BLOCKS, N], F32, name="result")
+        for k in range(BLOCKS):
+            product = psum.tile([128, N], F32, name=f"product{k}")
+            nc.tensor.matmul(product[:], weights_of_block[:, k, :], x[:], start=True, stop=True)
+            if k % 2 == 0:
+                nc.vector.tensor_scalar(result[:, k, :], product[:], bias[:, k : k + 1], 0.0, ADD, MAX)
+            else:
+                nc.scalar.activation(result[:, k, :], product[:], RELU, bias=bias[:, k : k + 1])
+        nc.sync.dma_start(out.rearrange("(p k) j -> p k j", k=BLOCKS), result[:])

@@ -25,6 +25,11 @@ def tile_lookup_cell_sigtanh_relu_kernel(tc, tab, w, b, offs, out):
         nc.sync.dma_start(weights[:], w)
         nc.sync.dma_start(bias[:], b.rearrange("(p k) o -> p (k o)", k=BLOCKS))
 
+        warm_in = held.tile([128, 1], F32, name="warm_in")
+        warm_out = held.tile([128, 1], F32, name="warm_out")
+        nc.vector.memset(warm_in[:], 0.0)
+        nc.scalar.activation(warm_out[:], warm_in[:], SIGMOID)
+
         opened = held.tile([R, N], F32, name="opened")
         squashed = held.tile([R, N], F32, name="squashed")
         nc.scalar.activation(opened[:], gate[:].indirect(offsets[:]), SIGMOID)

@@ -8,6 +8,7 @@ RELU = mybir.ActivationFunctionType.Relu
 
 R, S, N, M = 128, 256, 128, 256
 BLOCKS = M // 128
+WARM_MATMULS = 20
 FLOPS = 2 * R * M * N
 
 
@@ -25,10 +26,13 @@ def tile_lookup_cell_sigtanh_relu_kernel(tc, tab, w, b, offs, out):
         nc.sync.dma_start(weights[:], w)
         nc.sync.dma_start(bias[:], b.rearrange("(p k) o -> p (k o)", k=BLOCKS))
 
-        warm_in = held.tile([128, 1], F32, name="warm_in")
+        zeros = held.tile([128, 128], BF16, name="zeros")
         warm_out = held.tile([128, 1], F32, name="warm_out")
-        nc.vector.memset(warm_in[:], 0.0)
-        nc.scalar.activation(warm_out[:], warm_in[:], SIGMOID)
+        warm_bank = psum.tile([128, 128], F32, name="warm_bank")
+        nc.vector.memset(zeros[:], 0.0)
+        nc.scalar.activation(warm_out[:], zeros[:, 0:1], SIGMOID)
+        for turn in range(WARM_MATMULS):
+            nc.tensor.matmul(warm_bank[:], zeros[:], zeros[:], start=True, stop=True)
 
         opened = held.tile([R, N], F32, name="opened")
         squashed = held.tile([R, N], F32, name="squashed")

import concourse.mybir as mybir

F32, BF16, U16 = mybir.dt.float32, mybir.dt.bfloat16, mybir.dt.uint16
ADD, MAX, MULT = mybir.AluOpType.add, mybir.AluOpType.max, mybir.AluOpType.mult
SIGMOID = mybir.ActivationFunctionType.Sigmoid
TANH = mybir.ActivationFunctionType.Tanh
RELU = mybir.ActivationFunctionType.Relu

R, S, N, M = 128, 256, 128, 256
BLOCKS = M // 128
WARM_MATMULS = 20
FLOPS = 2 * R * M * N


def tile_lookup_cell_sigtanh_relu_kernel(tc, tab, w, b, offs, out):
    nc = tc.nc
    with tc.tile_pool(name="held", bufs=1) as held, tc.psum_pool(name="psum", bufs=1) as psum:
        offsets = held.tile([128, N // 16], U16, name="offsets")
        gate = held.tile([R, S], F32, name="gate")
        state = held.tile([R, S], F32, name="state")
        weights = held.tile([R, M], BF16, name="weights")
        bias = held.tile([128, BLOCKS], F32, name="bias")
        nc.sync.dma_start(offsets[:], offs)
        nc.sync.dma_start(gate[:], tab[0])
        nc.sync.dma_start(state[:], tab[1])
        nc.sync.dma_start(weights[:], w)
        nc.sync.dma_start(bias[:], b.rearrange("(p k) o -> p (k o)", k=BLOCKS))

        zeros = held.tile([128, 128], BF16, name="zeros")
        warm_out = held.tile([128, 1], F32, name="warm_out")
        warm_bank = psum.tile([128, 128], F32, name="warm_bank")
        nc.vector.memset(zeros[:], 0.0)
        nc.scalar.activation(warm_out[:], zeros[:, 0:1], SIGMOID)
        for turn in range(WARM_MATMULS):
            nc.tensor.matmul(warm_bank[:], zeros[:], zeros[:], start=True, stop=True)

        opened = held.tile([R, N], F32, name="opened")
        squashed = held.tile([R, N], F32, name="squashed")
        nc.scalar.activation(opened[:], gate[:].indirect(offsets[:]), SIGMOID)
        nc.scalar.activation(squashed[:], state[:].indirect(offsets[:]), TANH)
        x = held.tile([R, N], BF16, name="x")
        nc.vector.tensor_tensor(x[:], opened[:], squashed[:], MULT)

        weights_of_block = weights[:].rearrange("r (p k) -> r k p", k=BLOCKS)
        result = held.tile([128, BLOCKS, N], F32, name="result")
        for k in range(BLOCKS):
            product = psum.tile([128, N], F32, name=f"product{k}")
            nc.tensor.matmul(product[:], weights_of_block[:, k, :], x[:], start=True, stop=True)
            if k % 2 == 0:
                nc.vector.tensor_scalar(result[:, k, :], product[:], bias[:, k : k + 1], 0.0, ADD, MAX)
            else:
                nc.scalar.activation(result[:, k, :], product[:], RELU, bias=bias[:, k : k + 1])
        nc.sync.dma_start(out.rearrange("(p k) j -> p k j", k=BLOCKS), result[:])
